import numpy as np
import ml_dtypes


def mxq(x, axis, fmt="e4m3"):
    dtype, down = {"e4m3": (ml_dtypes.float8_e4m3fn, 7), "e5m2": (ml_dtypes.float8_e5m2, 14)}[fmt]
    v = np.moveaxis(np.asarray(x, np.float32).astype(ml_dtypes.bfloat16).astype(np.float64), axis, -1)
    blocks = v.reshape(v.shape[:-1] + (-1, 32))
    amax = np.abs(blocks).max(-1, keepdims=True)
    byte = np.maximum(np.where(amax > 0, np.frexp(amax)[1] - 1 + 127, 0) - down, 1)
    scale = np.exp2(byte - 127.0)
    codes = (blocks / scale).astype(np.float32).astype(dtype).astype(np.float64)
    return np.moveaxis((codes * scale).reshape(v.shape), -1, axis)


WIDE = False


def mx_kscale(k):
    if not WIDE:
        return np.ones(k)
    levels = np.array([10, -10, 5, -5, 0])
    if k % 512:
        return np.exp2(np.random.permutation(np.resize(levels, k // 32))).repeat(32)
    a = np.empty((k // 512, 16))
    for p in range(k // 512):
        a[p, :8] = np.random.permutation(np.resize(levels, 8))
        for g in range(8):
            far = levels[np.abs(levels - a[p, g]) >= 10]
            a[p, g + 8] = far[np.random.randint(len(far))]
    return np.exp2(a.ravel()).repeat(32)


def f64(x):
    return np.asarray(x).astype(np.float64)


def striped(idx):
    return np.tile(idx.reshape(-1, 16).T, (8, 1)).astype(np.uint16)


def unstriped(offs):
    return offs[:16].T.reshape(-1).astype(np.int64)


def pack_weight(w):
    k, n = w.shape
    w = f64(np.asarray(w, np.float32).astype(ml_dtypes.bfloat16)).reshape(k // 32, 32, n)
    amax = np.abs(w).max(1)
    byte = np.clip(np.where(amax > 0, np.frexp(amax)[1] - 1 + 127 - 7, 1), 1, 254)
    scaled = (w * np.exp2(127.0 - byte)[:, None, :]).reshape(k, n).astype(np.float32)
    words = np.ascontiguousarray(scaled.reshape(k // 512, 128, 4, n).transpose(0, 1, 3, 2)).astype(ml_dtypes.float8_e4m3fn).view(np.uint8)
    return words, np.ascontiguousarray(byte.astype(np.uint8).reshape(k // 512, 16, n))


def unpack_weight(words, scales):
    g, p, n, _ = words.shape
    vals = np.ascontiguousarray(words).view(ml_dtypes.float8_e4m3fn).astype(np.float64) * np.repeat(np.exp2(scales.astype(np.float64) - 127.0), 8, axis=1)[..., None]
    return vals.transpose(0, 1, 3, 2).reshape(g * 512, n)


K, T, E, C, N = 512, 2048, 8, 128, 512


def by_expert(wq, xq):
    return np.concatenate([wq[e].T @ xq[:, e * C:(e + 1) * C] for e in range(E)], axis=1)


def setup_inputs():
    n = np.random.standard_normal
    s = mx_kscale(K)[:, None]
    packed = [pack_weight(m) for m in n((E, K, N)) / np.sqrt(K) / s[None]]
    return {
        "xT": (n((K, T)) * s).astype(np.float32),
        "w_words": np.stack([m[0] for m in packed]),
        "w_scales": np.stack([m[1] for m in packed]),
        "gate": np.tile(np.random.uniform(0.2, 1.0, E * C), (N, 1)).astype(np.float32),
        "offs": striped(np.random.permutation(T)[:E * C]),
    }


def reference(xT, w_words, w_scales, gate, offs):
    idx = unstriped(offs)
    xq = mxq(f64(xT)[:, idx], 0, "e4m3")
    w = np.stack([unpack_weight(w_words[e], w_scales[e]) for e in range(E)])
    y = by_expert(w, xq)
    out = np.zeros((N, T))
    out[:, idx] = f64(gate) * y
    return out

@@ -1,0 +1,135 @@
+from contextlib import ExitStack
+
+import concourse.mybir as mybir
+
+K, T, E, C, N = 512, 2048, 8, 128, 512
+S = E * C
+
+FLOPS = 2 * K * N * S
+BYTES = K * S * 4 + E * K * N + E * (K // 32) * N + S * 4 + S * 2 + N * T * 4
+
+F32 = mybir.dt.float32
+BF16 = mybir.dt.bfloat16
+U32 = mybir.dt.uint32
+I32 = mybir.dt.int32
+U16 = mybir.dt.uint16
+U8 = mybir.dt.uint8
+FP8X4 = mybir.dt.float8_e4m3fn_x4
+MULT = mybir.AluOpType.mult
+
+P = 128
+SL = 256
+NSL = S // SL
+BK = 512
+NT = N // P
+LOADS = (
+    (0, 0, 1024, (("v", 0, 672), ("s", 672, 352))),
+    (0, 1024, 1024, (("v", 0, 672), ("s", 672, 352))),
+    (1, 0, 1024, (("s", 0, 640), ("g", 640, 384))),
+    (1, 1024, 512, (("v", 0, 512),)),
+    (1, 1536, 512, (("v", 0, 352), ("s", 352, 160))),
+)
+
+
+def tile_routed_moe_kernel(tc, xT, w_words, w_scales, gate, offs, out):
+    nc = tc.nc
+    with ExitStack() as ctx:
+        keep = ctx.enter_context(tc.tile_pool(name="keep", bufs=1))
+        wins = ctx.enter_context(tc.tile_pool(name="wins", bufs=3))
+        psum = ctx.enter_context(tc.psum_pool(name="psum", bufs=1))
+
+        offs_t = keep.tile([P, S // 16], U16, name="offs_t")
+
+        xv = xT.rearrange("(p t) n -> p t n", t=4)
+        raw = []
+        for i, (u, c0, cw, shares) in enumerate(LOADS):
+            raw.append(keep.tile([P, 2, cw], F32, name="raw%d" % i))
+            nc.sync.dma_start(raw[i][:], xv[:, 2 * u : 2 * u + 2, c0 : c0 + cw])
+            if i == 0:
+                nc.sync.dma_start(offs_t[:], offs)
+
+        wsc = keep.tile([P, E, N], U8, name="wsc", align_bytes=64)
+        nc.vector.memset(wsc[:].rearrange("p e n -> p (e n)").bitcast(I32), 0)
+        sv = w_scales.rearrange("e a q n -> q (e a) n").bitcast(I32)
+        for q in range(4):
+            nc.sync.dma_start(wsc[32 * q : 32 * q + 4, :, :].bitcast(I32), sv[4 * q : 4 * q + 4, :, :])
+
+        wv = w_words.rearrange("e a p n r -> p (e a) (n r)").bitcast(I32)
+        gate_t = keep.tile([P, S], F32, name="gate_t")
+        wt = {}
+        for h in range(2):
+            wt[0, h] = keep.tile([P, E // 2, P], I32, name="wt0_%d" % h, align_bytes=64)
+            nc.sync.dma_start(wt[0, h][:], wv[:, h * (E // 2) : (h + 1) * (E // 2), 0:P])
+            nc.sync.dma_start(gate_t[:, h * BK : (h + 1) * BK], gate[0:P, h * BK : (h + 1) * BK])
+        for nt in range(1, NT):
+            whole = keep.tile([P, E, P], I32, name="wt%d" % nt, align_bytes=64)
+            nc.sync.dma_start(whole[:], wv[:, :, nt * P : (nt + 1) * P])
+            wt[nt, 0] = whole[:, 0 : E // 2, :]
+            wt[nt, 1] = whole[:, E // 2 : E, :]
+
+        pair = [keep.tile([P, 2 * T], BF16, name="pair%d" % u) for u in range(2)]
+        for i, (u, c0, cw, shares) in enumerate(LOADS):
+            for eng, a, n in shares:
+                dst = pair[u][:, 2 * (c0 + a) : 2 * (c0 + a + n)].rearrange("p (w j) -> p w j", j=2)
+                src = raw[i][:, :, a : a + n].rearrange("p j w -> p w j")
+                if eng == "s":
+                    nc.scalar.copy(out=dst, in_=src)
+                elif eng == "g":
+                    nc.gpsimd.tensor_scalar(out=dst, in0=src, scalar1=1.0, scalar2=0.0, op0=MULT, op1=mybir.AluOpType.add)
+                else:
+                    nc.vector.tensor_copy(out=dst, in_=src)
+
+        gw = [keep.tile([P, 2, SL], U32, name="gw%d" % s) for s in range(NSL)]
+        xg = [keep.tile([P, 4 * SL], BF16, name="xg%d" % s, align_bytes=64) for s in range(NSL)]
+        xc = [keep.tile([P, SL], U32, name="xc%d" % s, align_bytes=64) for s in range(NSL)]
+        xs = [keep.tile([P, SL], U8, name="xs%d" % s, align_bytes=64) for s in range(NSL)]
+
+        def gather(u, s):
+            nc.vector.tensor_copy(
+                out=gw[s][:, u, :],
+                in_=pair[u][:].bitcast(U32).indirect(offs_t[:, s * (SL // 16) : (s + 1) * (SL // 16)]),
+            )
+
+        for s in range(NSL):
+            gather(0, s)
+        for s in range(NSL):
+            gather(1, s)
+            nc.scalar.copy(
+                out=xg[s][:].bitcast(U32).rearrange("p (n u) -> p n u", u=2),
+                in_=gw[s][:].rearrange("p u n -> p n u"),
+            )
+            nc.vector.quantize_mx(out=xc[s][:].bitcast(FP8X4), scales=xs[s][:], in_=xg[s][:])
+
+        for nt in range(NT):
+            win = wins.tile([P, T], F32, name="win")
+            if nt == 0:
+                nc.vector.memset(win[:], 0.0)
+            else:
+                nc.gpsimd.memset(win[:], 0.0)
+            y = keep.tile([P, S], F32, name="y%d" % nt)
+            for b in range(S // BK):
+                acc = psum.tile([P, BK], F32, name="acc%d_%d" % (nt, b))
+                for j in range(BK // C):
+                    e = b * (BK // C) + j
+                    s, o = divmod(e * C, SL)
+                    nc.tensor.matmul_mx(
+                        out=acc[:, j * C : (j + 1) * C],
+                        lhsT=wt[nt, b][:, j, :].bitcast(FP8X4),
+                        lhsT_scale=wsc[:, e, nt * P : (nt + 1) * P],
+                        rhs=xc[s][:, o : o + C].bitcast(FP8X4),
+                        rhs_scale=xs[s][:, o : o + C],
+                        start=True,
+                        stop=True,
+                    )
+                    if nt == 0 and b == 0 and j == 1:
+                        nc.scalar.copy(out=y[:, 0 : 2 * C], in_=acc[:, 0 : 2 * C])
+                if nt == 0 and b == 0:
+                    nc.scalar.copy(out=y[:, 2 * C : BK], in_=acc[:, 2 * C : BK])
+                else:
+                    nc.scalar.copy(out=y[:, b * BK : (b + 1) * BK], in_=acc[:])
+            cuts = (0, 256, 512, 1024) if nt == 0 else (0, 1024)
+            for a, z in zip(cuts[:-1], cuts[1:]):
+                nc.vector.tensor_tensor(
+                    out=win[:].indirect(offs_t[:, a // 16 : z // 16]), in0=y[:, a:z], in1=gate_t[:, a:z], op=MULT
+                )
+            nc.sync.dma_start(out[nt * P : (nt + 1) * P, :], win[:])

@@ -79,24 +79,20 @@ def tile_routed_moe_kernel(tc, xT, w_words, w_scales, gate, offs, out):
                 else:
                     nc.vector.tensor_copy(out=dst, in_=src)
 
-        gw = [keep.tile([P, 2, SL], U32, name="gw%d" % s) for s in range(NSL)]
+        gw = keep.tile([P, 2, S], U32, name="gw")
         xg = [keep.tile([P, 4 * SL], BF16, name="xg%d" % s, align_bytes=64) for s in range(NSL)]
         xc = [keep.tile([P, SL], U32, name="xc%d" % s, align_bytes=64) for s in range(NSL)]
         xs = [keep.tile([P, SL], U8, name="xs%d" % s, align_bytes=64) for s in range(NSL)]
 
-        def gather(u, s):
+        nc.vector.tensor_copy(out=gw[:, 0, :], in_=pair[0][:].bitcast(U32).indirect(offs_t[:]))
+        for s in range(NSL):
             nc.vector.tensor_copy(
-                out=gw[s][:, u, :],
-                in_=pair[u][:].bitcast(U32).indirect(offs_t[:, s * (SL // 16) : (s + 1) * (SL // 16)]),
+                out=gw[:, 1, s * SL : (s + 1) * SL],
+                in_=pair[1][:].bitcast(U32).indirect(offs_t[:, s * (SL // 16) : (s + 1) * (SL // 16)]),
             )
-
-        for s in range(NSL):
-            gather(0, s)
-        for s in range(NSL):
-            gather(1, s)
             nc.scalar.copy(
                 out=xg[s][:].bitcast(U32).rearrange("p (n u) -> p n u", u=2),
-                in_=gw[s][:].rearrange("p u n -> p n u"),
+                in_=gw[:, :, s * SL : (s + 1) * SL].rearrange("p u n -> p n u"),
             )
             nc.vector.quantize_mx(out=xc[s][:].bitcast(FP8X4), scales=xs[s][:], in_=xg[s][:])
 

@@ -123,7 +123,7 @@ def tile_routed_moe_kernel(tc, xT, w_words, w_scales, gate, offs, out):
                     nc.scalar.copy(out=y[:, 2 * C : BK], in_=acc[:, 2 * C : BK])
                 else:
                     nc.scalar.copy(out=y[:, b * BK : (b + 1) * BK], in_=acc[:])
-            cuts = (0, 256, 512, 1024) if nt == 0 else (0, 1024)
+            cuts = (0, 256, 1024) if nt == 0 else (0, 1024)
             for a, z in zip(cuts[:-1], cuts[1:]):
                 nc.vector.tensor_tensor(
                     out=win[:].indirect(offs_t[:, a // 16 : z // 16]), in0=y[:, a:z], in1=gate_t[:, a:z], op=MULT

@@ -27,7 +27,8 @@ LOADS = (
     (0, 1024, 1024, (("v", 0, 672), ("s", 672, 352))),
     (1, 0, 1024, (("s", 0, 640), ("g", 640, 384))),
     (1, 1024, 512, (("v", 0, 512),)),
-    (1, 1536, 512, (("v", 0, 352), ("s", 352, 160))),
+    (1, 1536, 256, (("v", 0, 256),)),
+    (1, 1792, 256, (("v", 0, 256),)),
 )
 
 

@@ -129,4 +129,8 @@ def tile_routed_moe_kernel(tc, xT, w_words, w_scales, gate, offs, out):
                 nc.vector.tensor_tensor(
                     out=win[:].indirect(offs_t[:, a // 16 : z // 16]), in0=y[:, a:z], in1=gate_t[:, a:z], op=MULT
                 )
-            nc.sync.dma_start(out[nt * P : (nt + 1) * P, :], win[:])
+            if nt < NT - 1:
+                nc.sync.dma_start(out[nt * P : (nt + 1) * P, :], win[:])
+            else:
+                nc.sync.dma_start(out[nt * P : (nt + 1) * P, 0 : T // 2], win[:, 0 : T // 2])
+                nc.scalar.dma_start(out[nt * P : (nt + 1) * P, T // 2 : T], win[:, T // 2 : T])

@@ -49,16 +49,16 @@ def tile_routed_moe_kernel(tc, xT, w_words, w_scales, gate, offs, out):
             if i == 0:
                 nc.sync.dma_start(offs_t[:], offs)
 
-        wsc = keep.tile([P, E, N], U8, name="wsc", align_bytes=64)
-        nc.vector.memset(wsc[:].rearrange("p e n -> p (e n)").bitcast(I32), 0)
-        sv = w_scales.rearrange("e a q n -> q (e a) n").bitcast(I32)
-        for q in range(4):
-            nc.sync.dma_start(wsc[32 * q : 32 * q + 4, :, :].bitcast(I32), sv[4 * q : 4 * q + 4, :, :])
+        wsc = keep.tile([P, E // 4, N], U8, name="wsc", align_bytes=64)
+        nc.vector.memset(wsc[:].rearrange("p g n -> p (g n)").bitcast(I32), 0)
 
         wv = w_words.rearrange("e a p n r -> p (e a) (n r)").bitcast(I32)
         gate_t = keep.tile([P, S], F32, name="gate_t")
         wt = {}
         for h in range(2):
+            sv = w_scales[4 * h : 4 * h + 4, 0, :, :].bitcast(I32)
+            for q in range(4):
+                nc.sync.dma_start(wsc[32 * q : 32 * q + 16, h, :].bitcast(I32), sv[:, 4 * q : 4 * q + 4, :])
             wt[0, h] = keep.tile([P, E // 2, P], I32, name="wt0_%d" % h, align_bytes=64)
             nc.sync.dma_start(wt[0, h][:], wv[:, h * (E // 2) : (h + 1) * (E // 2), 0:P])
             nc.sync.dma_start(gate_t[:, h * BK : (h + 1) * BK], gate[0:P, h * BK : (h + 1) * BK])
@@ -112,7 +112,7 @@ def tile_routed_moe_kernel(tc, xT, w_words, w_scales, gate, offs, out):
                     nc.tensor.matmul_mx(
                         out=acc[:, j * C : (j + 1) * C],
                         lhsT=wt[nt, b][:, j, :].bitcast(FP8X4),
-                        lhsT_scale=wsc[:, e, nt * P : (nt + 1) * P],
+                        lhsT_scale=wsc[4 * (e % 4) : P, e // 4, nt * P : (nt + 1) * P],
                         rhs=xc[s][:, o : o + C].bitcast(FP8X4),
                         rhs_scale=xs[s][:, o : o + C],
                         start=True,

@@ -36,7 +36,6 @@ def tile_routed_moe_kernel(tc, xT, w_words, w_scales, gate, offs, out):
     nc = tc.nc
     with ExitStack() as ctx:
         keep = ctx.enter_context(tc.tile_pool(name="keep", bufs=1))
-        wins = ctx.enter_context(tc.tile_pool(name="wins", bufs=3))
         psum = ctx.enter_context(tc.psum_pool(name="psum", bufs=1))
 
         offs_t = keep.tile([P, S // 16], U16, name="offs_t")
@@ -97,12 +96,11 @@ def tile_routed_moe_kernel(tc, xT, w_words, w_scales, gate, offs, out):
             )
             nc.vector.quantize_mx(out=xc[s][:].bitcast(FP8X4), scales=xs[s][:], in_=xg[s][:])
 
+        wins = [keep.tile([P, T], F32, name="win%d" % i) for i in range(2)]
+        nc.vector.memset(wins[0][:], 0.0)
+        nc.gpsimd.memset(wins[1][:], 0.0)
         for nt in range(NT):
-            win = wins.tile([P, T], F32, name="win")
-            if nt == 0:
-                nc.vector.memset(win[:], 0.0)
-            else:
-                nc.gpsimd.memset(win[:], 0.0)
+            win = wins[nt % 2]
             y = keep.tile([P, S], F32, name="y%d" % nt)
             for b in range(S // BK):
                 acc = psum.tile([P, BK], F32, name="acc%d_%d" % (nt, b))

@@ -23,8 +23,8 @@ NSL = S // SL
 BK = 512
 NT = N // P
 LOADS = (
-    (0, 0, 1024, (("v", 0, 672), ("s", 672, 352))),
-    (0, 1024, 1024, (("v", 0, 672), ("s", 672, 352))),
+    (0, 0, 1408, (("v", 0, 928), ("s", 928, 480))),
+    (0, 1408, 640, (("v", 0, 416), ("s", 416, 224))),
     (1, 0, 1024, (("s", 0, 640), ("g", 640, 384))),
     (1, 1024, 512, (("v", 0, 512),)),
     (1, 1536, 256, (("v", 0, 256),)),

@@ -96,37 +96,49 @@ def tile_routed_moe_kernel(tc, xT, w_words, w_scales, gate, offs, out):
             )
             nc.vector.quantize_mx(out=xc[s][:].bitcast(FP8X4), scales=xs[s][:], in_=xg[s][:])
 
-        wins = [keep.tile([P, T], F32, name="win%d" % i) for i in range(2)]
+        wins = [keep.tile([P, T], F32, name="win%d" % i) for i in range(3)]
         nc.vector.memset(wins[0][:], 0.0)
         nc.gpsimd.memset(wins[1][:], 0.0)
-        for nt in range(NT):
-            win = wins[nt % 2]
-            y = keep.tile([P, S], F32, name="y%d" % nt)
-            for b in range(S // BK):
-                acc = psum.tile([P, BK], F32, name="acc%d_%d" % (nt, b))
-                for j in range(BK // C):
-                    e = b * (BK // C) + j
+        nc.gpsimd.memset(wins[2][:], 0.0)
+        window_of = (wins[0], wins[1], wins[2], wins[1])
+
+        def multiply(nt, first, count, y):
+            done = 0
+            while done < count:
+                lo = first + done
+                n = min(count - done, BK - lo % BK)
+                tag = "bank%d_%d" % (1 if first else nt, lo // BK) if count > SL else "bank_first"
+                bank = psum.tile([P, BK], F32, name="acc%d_%d" % (nt, lo), tag=tag)
+                for e in range(lo // C, (lo + n) // C):
                     s, o = divmod(e * C, SL)
+                    c = e * C % BK
                     nc.tensor.matmul_mx(
-                        out=acc[:, j * C : (j + 1) * C],
-                        lhsT=wt[nt, b][:, j, :].bitcast(FP8X4),
+                        out=bank[:, c : c + C],
+                        lhsT=wt[nt, e // 4][:, e % 4, :].bitcast(FP8X4),
                         lhsT_scale=wsc[4 * (e % 4) : P, e // 4, nt * P : (nt + 1) * P],
                         rhs=xc[s][:, o : o + C].bitcast(FP8X4),
                         rhs_scale=xs[s][:, o : o + C],
                         start=True,
                         stop=True,
                     )
-                    if nt == 0 and b == 0 and j == 1:
-                        nc.scalar.copy(out=y[:, 0 : 2 * C], in_=acc[:, 0 : 2 * C])
-                if nt == 0 and b == 0:
-                    nc.scalar.copy(out=y[:, 2 * C : BK], in_=acc[:, 2 * C : BK])
-                else:
-                    nc.scalar.copy(out=y[:, b * BK : (b + 1) * BK], in_=acc[:])
-            cuts = (0, 256, 1024) if nt == 0 else (0, 1024)
-            for a, z in zip(cuts[:-1], cuts[1:]):
-                nc.vector.tensor_tensor(
-                    out=win[:].indirect(offs_t[:, a // 16 : z // 16]), in0=y[:, a:z], in1=gate_t[:, a:z], op=MULT
-                )
+                nc.scalar.copy(out=y[:, done : done + n], in_=bank[:, lo % BK : lo % BK + n])
+                done += n
+
+        def scatter(nt, first, count, y):
+            nc.vector.tensor_tensor(
+                out=window_of[nt][:].indirect(offs_t[:, first // 16 : (first + count) // 16]),
+                in0=y[:],
+                in1=gate_t[:, first : first + count],
+                op=MULT,
+            )
+
+        for nt, first, count in ((0, 0, SL), (1, 0, S), (2, 0, S), (0, SL, S - SL), (3, 0, S)):
+            y = keep.tile([P, count], F32, name="y%d_%d" % (nt, first))
+            multiply(nt, first, count, y)
+            scatter(nt, first, count, y)
+            if first + count < S:
+                continue
+            win = window_of[nt]
             if nt < NT - 1:
                 nc.sync.dma_start(out[nt * P : (nt + 1) * P, :], win[:])
             else:

@@ -53,19 +53,26 @@ def tile_routed_moe_kernel(tc, xT, w_words, w_scales, gate, offs, out):
 
         wv = w_words.rearrange("e a p n r -> p (e a) (n r)").bitcast(I32)
         gate_t = keep.tile([P, S], F32, name="gate_t")
-        wt = {}
+        codes = {}
+
+        def load_codes(nt, e0, e1):
+            t = keep.tile([P, e1 - e0, P], I32, name="codes%d_%d" % (nt, e0), align_bytes=64)
+            nc.sync.dma_start(t[:], wv[:, e0:e1, nt * P : (nt + 1) * P])
+            for e in range(e0, e1):
+                codes[nt, e] = t[:, e - e0, :]
+
         for h in range(2):
             sv = w_scales[4 * h : 4 * h + 4, 0, :, :].bitcast(I32)
             for q in range(4):
                 nc.sync.dma_start(wsc[32 * q : 32 * q + 16, h, :].bitcast(I32), sv[:, 4 * q : 4 * q + 4, :])
-            wt[0, h] = keep.tile([P, E // 2, P], I32, name="wt0_%d" % h, align_bytes=64)
-            nc.sync.dma_start(wt[0, h][:], wv[:, h * (E // 2) : (h + 1) * (E // 2), 0:P])
+            if h == 0:
+                load_codes(0, 0, SL // C)
+            else:
+                load_codes(1, 0, E)
             nc.sync.dma_start(gate_t[:, h * BK : (h + 1) * BK], gate[0:P, h * BK : (h + 1) * BK])
-        for nt in range(1, NT):
-            whole = keep.tile([P, E, P], I32, name="wt%d" % nt, align_bytes=64)
-            nc.sync.dma_start(whole[:], wv[:, :, nt * P : (nt + 1) * P])
-            wt[nt, 0] = whole[:, 0 : E // 2, :]
-            wt[nt, 1] = whole[:, E // 2 : E, :]
+        load_codes(0, SL // C, E)
+        load_codes(2, 0, E)
+        load_codes(3, 0, E)
 
         pair = [keep.tile([P, 2 * T], BF16, name="pair%d" % u) for u in range(2)]
         for i, (u, c0, cw, shares) in enumerate(LOADS):
@@ -114,7 +121,7 @@ def tile_routed_moe_kernel(tc, xT, w_words, w_scales, gate, offs, out):
                     c = e * C % BK
                     nc.tensor.matmul_mx(
                         out=bank[:, c : c + C],
-                        lhsT=wt[nt, e // 4][:, e % 4, :].bitcast(FP8X4),
+                        lhsT=codes[nt, e].bitcast(FP8X4),
                         lhsT_scale=wsc[4 * (e % 4) : P, e // 4, nt * P : (nt + 1) * P],
                         rhs=xc[s][:, o : o + C].bitcast(FP8X4),
                         rhs_scale=xs[s][:, o : o + C],

@@ -28,7 +28,8 @@ LOADS = (
     (1, 0, 1024, (("s", 0, 640), ("g", 640, 384))),
     (1, 1024, 512, (("v", 0, 512),)),
     (1, 1536, 256, (("v", 0, 256),)),
-    (1, 1792, 256, (("v", 0, 256),)),
+    (1, 1792, 128, (("v", 0, 128),)),
+    (1, 1920, 128, (("v", 0, 128),)),
 )
 
 
@@ -61,15 +62,18 @@ def tile_routed_moe_kernel(tc, xT, w_words, w_scales, gate, offs, out):
             for e in range(e0, e1):
                 codes[nt, e] = t[:, e - e0, :]
 
-        for h in range(2):
-            sv = w_scales[4 * h : 4 * h + 4, 0, :, :].bitcast(I32)
+        def load_scales(g):
+            rows = w_scales[4 * g : 4 * g + 4, 0, :, :].bitcast(I32)
             for q in range(4):
-                nc.sync.dma_start(wsc[32 * q : 32 * q + 16, h, :].bitcast(I32), sv[:, 4 * q : 4 * q + 4, :])
-            if h == 0:
-                load_codes(0, 0, SL // C)
-            else:
-                load_codes(1, 0, E)
-            nc.sync.dma_start(gate_t[:, h * BK : (h + 1) * BK], gate[0:P, h * BK : (h + 1) * BK])
+                nc.sync.dma_start(wsc[32 * q : 32 * q + 16, g, :].bitcast(I32), rows[:, 4 * q : 4 * q + 4, :])
+
+        load_scales(0)
+        load_codes(0, 0, SL // C)
+        load_codes(1, 0, E // 2)
+        nc.sync.dma_start(gate_t[:, 0:SL], gate[0:P, 0:SL])
+        load_scales(1)
+        load_codes(1, E // 2, E)
+        nc.sync.dma_start(gate_t[:, SL:S], gate[0:P, SL:S])
         load_codes(0, SL // C, E)
         load_codes(2, 0, E)
         load_codes(3, 0, E)

from contextlib import ExitStack

import concourse.mybir as mybir

K, T, E, C, N = 512, 2048, 8, 128, 512
S = E * C

FLOPS = 2 * K * N * S
BYTES = K * S * 4 + E * K * N + E * (K // 32) * N + S * 4 + S * 2 + N * T * 4

F32 = mybir.dt.float32
BF16 = mybir.dt.bfloat16
U32 = mybir.dt.uint32
I32 = mybir.dt.int32
U16 = mybir.dt.uint16
U8 = mybir.dt.uint8
FP8X4 = mybir.dt.float8_e4m3fn_x4
MULT = mybir.AluOpType.mult

P = 128
SL = 256
NSL = S // SL
BK = 512
NT = N // P
LOADS = (
    (0, 0, 1408, (("v", 0, 928), ("s", 928, 480))),
    (0, 1408, 640, (("v", 0, 416), ("s", 416, 224))),
    (1, 0, 1024, (("s", 0, 640), ("g", 640, 384))),
    (1, 1024, 512, (("v", 0, 512),)),
    (1, 1536, 256, (("v", 0, 256),)),
    (1, 1792, 128, (("v", 0, 128),)),
    (1, 1920, 128, (("v", 0, 128),)),
)


def tile_routed_moe_kernel(tc, xT, w_words, w_scales, gate, offs, out):
    nc = tc.nc
    with ExitStack() as ctx:
        keep = ctx.enter_context(tc.tile_pool(name="keep", bufs=1))
        psum = ctx.enter_context(tc.psum_pool(name="psum", bufs=1))

        offs_t = keep.tile([P, S // 16], U16, name="offs_t")

        xv = xT.rearrange("(p t) n -> p t n", t=4)
        raw = []
        for i, (u, c0, cw, shares) in enumerate(LOADS):
            raw.append(keep.tile([P, 2, cw], F32, name="raw%d" % i))
            nc.sync.dma_start(raw[i][:], xv[:, 2 * u : 2 * u + 2, c0 : c0 + cw])
            if i == 0:
                nc.sync.dma_start(offs_t[:], offs)

        wsc = keep.tile([P, E // 4, N], U8, name="wsc", align_bytes=64)
        nc.vector.memset(wsc[:].rearrange("p g n -> p (g n)").bitcast(I32), 0)

        wv = w_words.rearrange("e a p n r -> p (e a) (n r)").bitcast(I32)
        gate_t = keep.tile([P, S], F32, name="gate_t")
        codes = {}

        def load_codes(nt, e0, e1):
            t = keep.tile([P, e1 - e0, P], I32, name="codes%d_%d" % (nt, e0), align_bytes=64)
            nc.sync.dma_start(t[:], wv[:, e0:e1, nt * P : (nt + 1) * P])
            for e in range(e0, e1):
                codes[nt, e] = t[:, e - e0, :]

        def load_scales(g):
            rows = w_scales[4 * g : 4 * g + 4, 0, :, :].bitcast(I32)
            for q in range(4):
                nc.sync.dma_start(wsc[32 * q : 32 * q + 16, g, :].bitcast(I32), rows[:, 4 * q : 4 * q + 4, :])

        load_scales(0)
        load_codes(0, 0, SL // C)
        load_codes(1, 0, E // 2)
        nc.sync.dma_start(gate_t[:, 0:SL], gate[0:P, 0:SL])
        load_scales(1)
        load_codes(1, E // 2, E)
        nc.sync.dma_start(gate_t[:, SL:S], gate[0:P, SL:S])
        load_codes(0, SL // C, E)
        load_codes(2, 0, E)
        load_codes(3, 0, E)

        pair = [keep.tile([P, 2 * T], BF16, name="pair%d" % u) for u in range(2)]
        for i, (u, c0, cw, shares) in enumerate(LOADS):
            for eng, a, n in shares:
                dst = pair[u][:, 2 * (c0 + a) : 2 * (c0 + a + n)].rearrange("p (w j) -> p w j", j=2)
                src = raw[i][:, :, a : a + n].rearrange("p j w -> p w j")
                if eng == "s":
                    nc.scalar.copy(out=dst, in_=src)
                elif eng == "g":
                    nc.gpsimd.tensor_scalar(out=dst, in0=src, scalar1=1.0, scalar2=0.0, op0=MULT, op1=mybir.AluOpType.add)
                else:
                    nc.vector.tensor_copy(out=dst, in_=src)

        gw = keep.tile([P, 2, S], U32, name="gw")
        xg = [keep.tile([P, 4 * SL], BF16, name="xg%d" % s, align_bytes=64) for s in range(NSL)]
        xc = [keep.tile([P, SL], U32, name="xc%d" % s, align_bytes=64) for s in range(NSL)]
        xs = [keep.tile([P, SL], U8, name="xs%d" % s, align_bytes=64) for s in range(NSL)]

        nc.vector.tensor_copy(out=gw[:, 0, :], in_=pair[0][:].bitcast(U32).indirect(offs_t[:]))
        for s in range(NSL):
            nc.vector.tensor_copy(
                out=gw[:, 1, s * SL : (s + 1) * SL],
                in_=pair[1][:].bitcast(U32).indirect(offs_t[:, s * (SL // 16) : (s + 1) * (SL // 16)]),
            )
            nc.scalar.copy(
                out=xg[s][:].bitcast(U32).rearrange("p (n u) -> p n u", u=2),
                in_=gw[:, :, s * SL : (s + 1) * SL].rearrange("p u n -> p n u"),
            )
            nc.vector.quantize_mx(out=xc[s][:].bitcast(FP8X4), scales=xs[s][:], in_=xg[s][:])

        wins = [keep.tile([P, T], F32, name="win%d" % i) for i in range(3)]
        nc.vector.memset(wins[0][:], 0.0)
        nc.gpsimd.memset(wins[1][:], 0.0)
        nc.gpsimd.memset(wins[2][:], 0.0)
        window_of = (wins[0], wins[1], wins[2], wins[1])

        def multiply(nt, first, count, y):
            done = 0
            while done < count:
                lo = first + done
                n = min(count - done, BK - lo % BK)
                tag = "bank%d_%d" % (1 if first else nt, lo // BK) if count > SL else "bank_first"
                bank = psum.tile([P, BK], F32, name="acc%d_%d" % (nt, lo), tag=tag)
                for e in range(lo // C, (lo + n) // C):
                    s, o = divmod(e * C, SL)
                    c = e * C % BK
                    nc.tensor.matmul_mx(
                        out=bank[:, c : c + C],
                        lhsT=codes[nt, e].bitcast(FP8X4),
                        lhsT_scale=wsc[4 * (e % 4) : P, e // 4, nt * P : (nt + 1) * P],
                        rhs=xc[s][:, o : o + C].bitcast(FP8X4),
                        rhs_scale=xs[s][:, o : o + C],
                        start=True,
                        stop=True,
                    )
                nc.scalar.copy(out=y[:, done : done + n], in_=bank[:, lo % BK : lo % BK + n])
                done += n

        def scatter(nt, first, count, y):
            nc.vector.tensor_tensor(
                out=window_of[nt][:].indirect(offs_t[:, first // 16 : (first + count) // 16]),
                in0=y[:],
                in1=gate_t[:, first : first + count],
                op=MULT,
            )

        for nt, first, count in ((0, 0, SL), (1, 0, S), (2, 0, S), (0, SL, S - SL), (3, 0, S)):
            y = keep.tile([P, count], F32, name="y%d_%d" % (nt, first))
            multiply(nt, first, count, y)
            scatter(nt, first, count, y)
            if first + count < S:
                continue
            win = window_of[nt]
            if nt < NT - 1:
                nc.sync.dma_start(out[nt * P : (nt + 1) * P, :], win[:])
            else:
                nc.sync.dma_start(out[nt * P : (nt + 1) * P, 0 : T // 2], win[:, 0 : T // 2])
                nc.scalar.dma_start(out[nt * P : (nt + 1) * P, T // 2 : T], win[:, T // 2 : T])
